import numpy as np, ml_dtypes
CORES = [51,54,179,182]
N = 4
import mx_ref
NC, G = 256, 4
C = np.float32(0.031)
BF = ml_dtypes.bfloat16
def cut(t, i, w=512):
    return t[:, w * i:w * i + w]
def tile(rs):
    return np.stack(rs, axis=2).reshape(128, -1).astype(BF)
def layer(w, X):
    out = []
    for i in range(G):
        for t in range(len(X)):
            p = mx_ref.matmul(mx_ref.quantize(cut(w, len(X) * i + t)), X[t])
            z = p if t == 0 else z + p
        out.append(z)
    return out
def act(Z):
    return [np.maximum(z, 0) * C for z in Z]
def setup_inputs(rng):
    def f(*shape):
        return mx_ref.flush((rng.standard_normal(shape, dtype=np.float32) * np.exp2(rng.integers(-2, 3, shape[:-1] + (1,)))).astype(BF))
    return {"x": f(N, 128, 4 * NC), "w1": f(N, 128, G * 512), "w2": f(N, 128, 512)}
def setup_inputs_blocks(rng):
    d = setup_inputs(rng)
    for k in ("x", "w1", "w2"): d[k] = mx_ref.spread(d[k], rng, 2)
    return d
def setup_inputs_wide(rng):
    d = setup_inputs(rng)
    for k in ("x", "w1", "w2"): d[k] = mx_ref.flush((d[k].astype(np.float32) * np.exp2(rng.integers(-6, 7, (N, 1, 1))).astype(np.float32)).astype(BF))
    return d
def reference(x, w1, w2):
    X = [mx_ref.quantize(x[j]) for j in range(N)]
    y = np.zeros((N, 128, NC), np.float32)
    for c in range(N):
        for r in range(N):
            p = mx_ref.matmul(mx_ref.quantize(w2[r]), mx_ref.quantize(tile(act(layer(w1[r], [X[c]])))))
            y[c] = p if r == 0 else y[c] + p
    return {"y": y}

@@ -1,0 +1,186 @@
+from concourse.bass import DstId, RemoteDMATransfer
+from concourse.mybir import dt, AluOpType, ActivationFunctionType
+
+N = 4
+NC = 256
+TW = 128
+WC = 5 * TW
+KA = 3
+AC = KA * TW
+CSCALE = 0.031
+ZB = 7
+
+SCRATCH = {
+    "w1b": ("sbuf", [128, 4 * 4 * TW], "bfloat16"),
+    "w2b": ("sbuf", [128, 4 * TW], "bfloat16"),
+    "xb": ("sbuf", [128, 4 * NC], "bfloat16"),
+    "xq": ("sbuf", [128, NC], "float8_e4m3fn_x4"),
+    "xs": ("sbuf", [128, NC], "uint8"),
+    "wq": ("sbuf", [128, N * WC], "float8_e4m3fn_x4"),
+    "ws": ("sbuf", [128, N * WC], "uint8"),
+    "hb": ("sbuf", [128, N * 4 * NC], "bfloat16"),
+    "hq": ("sbuf", [128, N * NC], "float8_e4m3fn_x4"),
+    "hs": ("sbuf", [128, N * NC], "uint8"),
+    "ysb": ("sbuf", [128, NC], "float32"),
+    "ps": ("psum", [128, 512 * (ZB + 1)], "float32"),
+}
+SEMAPHORES = (["lA", "lT", "lW", "lX", "qA", "qT", "qW", "qX", "ls", "yd", "cp", "st"]
+              + ["sA%d" % r for r in range(N)] + ["sS%d" % r for r in range(N)] + ["sB%d" % r for r in range(N)]
+              + ["z%d" % k for k in range(4 * N)] + ["a%d" % k for k in range(4 * N)] + ["hq%d" % r for r in range(N)])
+
+
+def _engines(mask):
+    return [e for e in range(mask.bit_length()) if (mask >> e) & 1]
+
+
+def _pack(engs):
+    m = 0
+    for e in engs:
+        m |= 1 << e
+    return m
+
+
+def _count(mask):
+    return len(_engines(mask))
+
+
+def _roles(c, cores, topo):
+    others = [o for o in cores if o != c]
+    nb = [o for o in others if topo.host(o) == topo.host(c) and topo.chip(o) == topo.chip(c)][0]
+    far = [o for o in others if o != nb]
+    peer = [o for o in far if topo.die(o) == topo.die(c)][0]
+    diag = [o for o in far if o != peer][0]
+    off = topo.mask(c, peer) & topo.mask(c, diag)
+    on = topo.mask(c, nb) & ~off
+    e = _engines(off)
+    return {"nb": nb, "peer": peer, "diag": diag, "off": off, "on": on,
+            "lo": _pack(e[:len(e) // 2]), "hi": _pack(e[len(e) // 2:])}
+
+
+def rank_program(g, core, T, topo):
+    me = T.rank_of(core)
+    if me is None:
+        return
+    S = T.sem
+    R = _roles(core, T.cores, topo)
+    nb, peer, diag = R["nb"], R["peer"], R["diag"]
+    rn, rp, rd = T.rank_of(nb), T.rank_of(peer), T.rank_of(diag)
+    v, sc, te = g.vector, g.scalar, g.tensor
+
+    def cod(r, a, b):
+        return T.wq[:, WC * r + a:WC * r + b]
+
+    def pla(r, a, b):
+        return T.ws[:, WC * r + a:WC * r + b]
+
+    ea = 4 * AC
+    g.sync.dma_start(T.w1b[0:64, 0:ea], T.w1[0:64, 0:ea]).then_inc(S.lA, 16)
+    sc.dma_start(T.w1b[64:128, 0:ea], T.w1[64:128, 0:ea]).then_inc(S.lA, 16)
+    g.sync.dma_start(T.w1b[:, ea:16 * TW], T.w1[:, ea:16 * TW]).then_inc(S.lT, 16)
+    sc.dma_start(T.w2b[:], T.w2[:]).then_inc(S.lW, 16)
+    g.sync.dma_start(T.xb[0:64, :], T.x[0:64, :]).then_inc(S.lX, 16)
+    sc.dma_start(T.xb[64:128, :], T.x[64:128, :]).then_inc(S.lX, 16)
+
+    v.wait_ge(S.lA, 32)
+    v.quantize_mx(cod(me, 0, AC), pla(me, 0, AC), T.w1b[:, 0:ea]).then_inc(S.qA, 1)
+    v.wait_ge(S.lT, 16)
+    v.quantize_mx(cod(me, AC, 4 * TW), pla(me, AC, 4 * TW), T.w1b[:, ea:16 * TW]).then_inc(S.qT, 1)
+    v.wait_ge(S.lW, 16)
+    v.quantize_mx(cod(me, 4 * TW, WC), pla(me, 4 * TW, WC), T.w2b[:]).then_inc(S.qW, 1)
+    v.wait_ge(S.lX, 32)
+    v.quantize_mx(T.xq[:], T.xs[:], T.xb[:]).then_inc(S.qX, 1)
+
+    sent = [0]
+
+    def xfer(dst, mask, sem, ap):
+        rid, pid = topo.addr(dst, core)
+        sent[0] += _count(mask)
+        return RemoteDMATransfer(dst_ids=[DstId(rid=rid, pnc=pid)], dma_engine_mask=mask, remote_sem=sem, src=ap, dst=ap)
+
+    a_own = cod(me, 0, AC).bitcast(dt.uint8)
+    b_own = cod(me, AC, WC).bitcast(dt.uint8)
+    s_own = pla(me, 0, WC)
+    g.wait_ge(S.qA, 1)
+    g.remote_dma_fused([xfer(peer, R["off"], S["sA%d" % me], a_own),
+                        xfer(nb, R["on"], S["sA%d" % me], a_own)], local_sem=S.ls)
+    g.wait_ge(S.qT, 1)
+    g.wait_ge(S.qW, 1)
+    g.remote_dma_fused([xfer(peer, R["lo"], S["sS%d" % me], s_own),
+                        xfer(diag, R["hi"], S["sS%d" % me], s_own),
+                        xfer(nb, R["on"], S["sS%d" % me], s_own)], local_sem=S.ls)
+    g.remote_dma_fused([xfer(peer, R["lo"], S["sB%d" % me], b_own),
+                        xfer(diag, R["hi"], S["sB%d" % me], b_own),
+                        xfer(nb, R["on"], S["sB%d" % me], b_own)], local_sem=S.ls)
+
+    Rn, Rp, Rd = _roles(nb, T.cores, topo), _roles(peer, T.cores, topo), _roles(diag, T.cores, topo)
+    need = {("A", rn): _count(Rn["on"]), ("S", rn): _count(Rn["on"]), ("B", rn): _count(Rn["on"]),
+            ("A", rp): _count(Rp["off"]), ("S", rp): _count(Rp["lo"]), ("B", rp): _count(Rp["lo"]),
+            ("A", rd): _count(Rn["on"]), ("S", rd): _count(Rd["hi"]), ("B", rd): _count(Rd["hi"])}
+
+    g.wait_ge(S["sA%d" % rp], need[("A", rp)])
+    a_peer = cod(rp, 0, AC).bitcast(dt.uint8)
+    g.remote_dma_fused([xfer(nb, R["on"], S["sA%d" % rp], a_peer)], local_sem=S.ls)
+    g.wait_ge(S.ls, sent[0])
+
+    seq = ([("Z", me, i) for i in range(4)] + [("Y", me, 0)]
+           + [("Z", rn, i) for i in range(KA)] + [("Z", rp, i) for i in range(KA)]
+           + [("Z", rn, i) for i in range(KA, 4)] + [("Y", rn, 0)]
+           + [("Z", rd, i) for i in range(KA)]
+           + [("Z", rp, i) for i in range(KA, 4)] + [("Z", rd, i) for i in range(KA, 4)]
+           + [("Y", rp, 0), ("Y", rd, 0)])
+    waited = set()
+
+    def twait(name, val):
+        if name not in waited:
+            waited.add(name)
+            te.wait_ge(S[name], val)
+
+    def operands(r, piece):
+        if r == me:
+            twait({"A": "qA", "T": "qT", "W": "qW"}[piece], 1)
+        else:
+            p = "A" if piece == "A" else "B"
+            twait("s%s%d" % (p, r), need[(p, r)])
+            twait("sS%d" % r, need[("S", r)])
+
+    k = 0
+    acts = {r: [] for r in range(N)}
+    ny = 0
+    ybank = T.ps[:, 512 * ZB:512 * ZB + NC]
+    for kind, r, i in seq:
+        if kind == "Z":
+            twait("qX", 1)
+            operands(r, "A" if i < KA else "T")
+            if k >= ZB:
+                twait("a%d" % (k - ZB), 1)
+            bank = T.ps[:, 512 * (k % ZB):512 * (k % ZB) + NC]
+            te.matmul_mx(bank, cod(r, TW * i, TW * i + TW), pla(r, TW * i, TW * i + TW),
+                         T.xq[:], T.xs[:], True, True).then_inc(S["z%d" % k], 1)
+            hv = T.hb[:, 4 * NC * r + i:4 * NC * (r + 1):4]
+            if i == 1:
+                v.wait_ge(S["z%d" % k], 1)
+                v.tensor_scalar(hv, bank, 0.0, CSCALE, AluOpType.max, AluOpType.mult).then_inc(S["a%d" % k], 1)
+            else:
+                sc.wait_ge(S["z%d" % k], 1)
+                sc.activation(hv, bank, ActivationFunctionType.Relu, scale=CSCALE).then_inc(S["a%d" % k], 1)
+            acts[r].append(k)
+            k += 1
+            if len(acts[r]) == 4:
+                for j in acts[r]:
+                    v.wait_ge(S["a%d" % j], 1)
+                v.quantize_mx(T.hq[:, NC * r:NC * (r + 1)], T.hs[:, NC * r:NC * (r + 1)],
+                              T.hb[:, 4 * NC * r:4 * NC * (r + 1)]).then_inc(S["hq%d" % r], 1)
+        else:
+            operands(r, "W")
+            twait("hq%d" % r, 1)
+            ny += 1
+            mm = te.matmul_mx(ybank, cod(r, 4 * TW, WC), pla(r, 4 * TW, WC),
+                              T.hq[:, NC * r:NC * (r + 1)], T.hs[:, NC * r:NC * (r + 1)], ny == 1, ny == N)
+            if ny == N:
+                mm.then_inc(S.yd, 1)
+
+    sc.wait_ge(S.yd, 1)
+    sc.activation(T.ysb[:], ybank, ActivationFunctionType.Copy).then_inc(S.cp, 1)
+    sc.wait_ge(S.cp, 1)
+    sc.dma_start(T.y[:], T.ysb[:]).then_inc(S.st, 16)
+    sc.wait_ge(S.st, 16)

@@ -24,8 +24,9 @@ SCRATCH = {
     "ysb": ("sbuf", [128, NC], "float32"),
     "ps": ("psum", [128, 512 * (ZB + 1)], "float32"),
 }
-SEMAPHORES = (["lA", "lT", "lW", "lX", "qA", "qT", "qW", "qX", "ls", "yd", "cp", "st"]
-              + ["sA%d" % r for r in range(N)] + ["sS%d" % r for r in range(N)] + ["sB%d" % r for r in range(N)]
+SEMAPHORES = (["lP", "lA", "lT", "lW", "lX", "qP", "qA", "qT", "qW", "qX", "ls", "yd", "cp", "st"]
+              + ["sP%d" % r for r in range(N)] + ["sA%d" % r for r in range(N)]
+              + ["sS%d" % r for r in range(N)] + ["sB%d" % r for r in range(N)]
               + ["z%d" % k for k in range(4 * N)] + ["a%d" % k for k in range(4 * N)] + ["hq%d" % r for r in range(N)])
 
 
@@ -73,16 +74,20 @@ def rank_program(g, core, T, topo):
     def pla(r, a, b):
         return T.ws[:, WC * r + a:WC * r + b]
 
-    ea = 4 * AC
-    g.sync.dma_start(T.w1b[0:64, 0:ea], T.w1[0:64, 0:ea]).then_inc(S.lA, 16)
-    sc.dma_start(T.w1b[64:128, 0:ea], T.w1[64:128, 0:ea]).then_inc(S.lA, 16)
+    e0, ea = 4 * TW, 4 * AC
+    g.sync.dma_start(T.w1b[0:64, 0:e0], T.w1[0:64, 0:e0]).then_inc(S.lP, 16)
+    sc.dma_start(T.w1b[64:128, 0:e0], T.w1[64:128, 0:e0]).then_inc(S.lP, 16)
+    g.sync.dma_start(T.w1b[0:64, e0:ea], T.w1[0:64, e0:ea]).then_inc(S.lA, 16)
+    sc.dma_start(T.w1b[64:128, e0:ea], T.w1[64:128, e0:ea]).then_inc(S.lA, 16)
     g.sync.dma_start(T.w1b[:, ea:16 * TW], T.w1[:, ea:16 * TW]).then_inc(S.lT, 16)
     sc.dma_start(T.w2b[:], T.w2[:]).then_inc(S.lW, 16)
     g.sync.dma_start(T.xb[0:64, :], T.x[0:64, :]).then_inc(S.lX, 16)
     sc.dma_start(T.xb[64:128, :], T.x[64:128, :]).then_inc(S.lX, 16)
 
+    v.wait_ge(S.lP, 32)
+    v.quantize_mx(cod(me, 0, TW), pla(me, 0, TW), T.w1b[:, 0:e0]).then_inc(S.qP, 1)
     v.wait_ge(S.lA, 32)
-    v.quantize_mx(cod(me, 0, AC), pla(me, 0, AC), T.w1b[:, 0:ea]).then_inc(S.qA, 1)
+    v.quantize_mx(cod(me, TW, AC), pla(me, TW, AC), T.w1b[:, e0:ea]).then_inc(S.qA, 1)
     v.wait_ge(S.lT, 16)
     v.quantize_mx(cod(me, AC, 4 * TW), pla(me, AC, 4 * TW), T.w1b[:, ea:16 * TW]).then_inc(S.qT, 1)
     v.wait_ge(S.lW, 16)
@@ -97,29 +102,36 @@ def rank_program(g, core, T, topo):
         sent[0] += _count(mask)
         return RemoteDMATransfer(dst_ids=[DstId(rid=rid, pnc=pid)], dma_engine_mask=mask, remote_sem=sem, src=ap, dst=ap)
 
-    a_own = cod(me, 0, AC).bitcast(dt.uint8)
+    p_own = cod(me, 0, TW).bitcast(dt.uint8)
+    a_own = cod(me, TW, AC).bitcast(dt.uint8)
     b_own = cod(me, AC, WC).bitcast(dt.uint8)
     s_own = pla(me, 0, WC)
+    g.wait_ge(S.qP, 1)
+    g.remote_dma_fused([xfer(peer, R["off"], S["sP%d" % me], p_own),
+                        xfer(nb, R["on"], S["sP%d" % me], p_own)], local_sem=S.ls)
     g.wait_ge(S.qA, 1)
     g.remote_dma_fused([xfer(peer, R["off"], S["sA%d" % me], a_own),
                         xfer(nb, R["on"], S["sA%d" % me], a_own)], local_sem=S.ls)
     g.wait_ge(S.qT, 1)
     g.wait_ge(S.qW, 1)
-    g.remote_dma_fused([xfer(peer, R["lo"], S["sS%d" % me], s_own),
-                        xfer(diag, R["hi"], S["sS%d" % me], s_own),
+    g.remote_dma_fused([xfer(peer, R["off"], S["sS%d" % me], s_own),
                         xfer(nb, R["on"], S["sS%d" % me], s_own)], local_sem=S.ls)
     g.remote_dma_fused([xfer(peer, R["lo"], S["sB%d" % me], b_own),
                         xfer(diag, R["hi"], S["sB%d" % me], b_own),
                         xfer(nb, R["on"], S["sB%d" % me], b_own)], local_sem=S.ls)
 
     Rn, Rp, Rd = _roles(nb, T.cores, topo), _roles(peer, T.cores, topo), _roles(diag, T.cores, topo)
-    need = {("A", rn): _count(Rn["on"]), ("S", rn): _count(Rn["on"]), ("B", rn): _count(Rn["on"]),
-            ("A", rp): _count(Rp["off"]), ("S", rp): _count(Rp["lo"]), ("B", rp): _count(Rp["lo"]),
-            ("A", rd): _count(Rn["on"]), ("S", rd): _count(Rd["hi"]), ("B", rd): _count(Rd["hi"])}
+    need = {("P", rn): _count(Rn["on"]), ("A", rn): _count(Rn["on"]), ("S", rn): _count(Rn["on"]), ("B", rn): _count(Rn["on"]),
+            ("P", rp): _count(Rp["off"]), ("A", rp): _count(Rp["off"]), ("S", rp): _count(Rp["off"]),
+            ("B", rp): _count(Rp["lo"]),
+            ("A", rd): _count(Rn["on"]), ("S", rd): _count(Rn["on"]), ("B", rd): _count(Rd["hi"])}
 
+    g.wait_ge(S["sP%d" % rp], need[("P", rp)])
     g.wait_ge(S["sA%d" % rp], need[("A", rp)])
     a_peer = cod(rp, 0, AC).bitcast(dt.uint8)
     g.remote_dma_fused([xfer(nb, R["on"], S["sA%d" % rp], a_peer)], local_sem=S.ls)
+    g.wait_ge(S["sS%d" % rp], need[("S", rp)])
+    g.remote_dma_fused([xfer(nb, R["on"], S["sS%d" % rp], pla(rp, 0, WC))], local_sem=S.ls)
     g.wait_ge(S.ls, sent[0])
 
     seq = ([("Z", me, i) for i in range(4)] + [("Y", me, 0)]
@@ -137,9 +149,11 @@ def rank_program(g, core, T, topo):
 
     def operands(r, piece):
         if r == me:
-            twait({"A": "qA", "T": "qT", "W": "qW"}[piece], 1)
+            twait({"P": "qP", "A": "qA", "T": "qT", "W": "qW"}[piece], 1)
         else:
-            p = "A" if piece == "A" else "B"
+            p = {"P": "P", "A": "A", "T": "B", "W": "B"}[piece]
+            if r == rd and p == "P":
+                p = "A"
             twait("s%s%d" % (p, r), need[(p, r)])
             twait("sS%d" % r, need[("S", r)])
 
@@ -150,7 +164,7 @@ def rank_program(g, core, T, topo):
     for kind, r, i in seq:
         if kind == "Z":
             twait("qX", 1)
-            operands(r, "A" if i < KA else "T")
+            operands(r, "P" if i == 0 else ("A" if i < KA else "T"))
             if k >= ZB:
                 twait("a%d" % (k - ZB), 1)
             bank = T.ps[:, 512 * (k % ZB):512 * (k % ZB) + NC]

@@ -25,8 +25,7 @@ SCRATCH = {
     "ps": ("psum", [128, 512 * (ZB + 1)], "float32"),
 }
 SEMAPHORES = (["lP", "lA", "lT", "lW", "lX", "qP", "qA", "qT", "qW", "qX", "ls", "yd", "cp", "st"]
-              + ["sP%d" % r for r in range(N)] + ["sA%d" % r for r in range(N)]
-              + ["sS%d" % r for r in range(N)] + ["sB%d" % r for r in range(N)]
+              + ["s%s%d" % (p, r) for p in "PASTW" for r in range(N)]
               + ["z%d" % k for k in range(4 * N)] + ["a%d" % k for k in range(4 * N)] + ["hq%d" % r for r in range(N)])
 
 
@@ -77,23 +76,23 @@ def rank_program(g, core, T, topo):
     e0, ea = 4 * TW, 4 * AC
     g.sync.dma_start(T.w1b[0:64, 0:e0], T.w1[0:64, 0:e0]).then_inc(S.lP, 16)
     sc.dma_start(T.w1b[64:128, 0:e0], T.w1[64:128, 0:e0]).then_inc(S.lP, 16)
+    g.sync.dma_start(T.xb[0:64, :], T.x[0:64, :]).then_inc(S.lX, 16)
+    sc.dma_start(T.xb[64:128, :], T.x[64:128, :]).then_inc(S.lX, 16)
     g.sync.dma_start(T.w1b[0:64, e0:ea], T.w1[0:64, e0:ea]).then_inc(S.lA, 16)
     sc.dma_start(T.w1b[64:128, e0:ea], T.w1[64:128, e0:ea]).then_inc(S.lA, 16)
     g.sync.dma_start(T.w1b[:, ea:16 * TW], T.w1[:, ea:16 * TW]).then_inc(S.lT, 16)
     sc.dma_start(T.w2b[:], T.w2[:]).then_inc(S.lW, 16)
-    g.sync.dma_start(T.xb[0:64, :], T.x[0:64, :]).then_inc(S.lX, 16)
-    sc.dma_start(T.xb[64:128, :], T.x[64:128, :]).then_inc(S.lX, 16)
 
     v.wait_ge(S.lP, 32)
     v.quantize_mx(cod(me, 0, TW), pla(me, 0, TW), T.w1b[:, 0:e0]).then_inc(S.qP, 1)
+    v.wait_ge(S.lX, 32)
+    v.quantize_mx(T.xq[:], T.xs[:], T.xb[:]).then_inc(S.qX, 1)
     v.wait_ge(S.lA, 32)
     v.quantize_mx(cod(me, TW, AC), pla(me, TW, AC), T.w1b[:, e0:ea]).then_inc(S.qA, 1)
     v.wait_ge(S.lT, 16)
     v.quantize_mx(cod(me, AC, 4 * TW), pla(me, AC, 4 * TW), T.w1b[:, ea:16 * TW]).then_inc(S.qT, 1)
     v.wait_ge(S.lW, 16)
     v.quantize_mx(cod(me, 4 * TW, WC), pla(me, 4 * TW, WC), T.w2b[:]).then_inc(S.qW, 1)
-    v.wait_ge(S.lX, 32)
-    v.quantize_mx(T.xq[:], T.xs[:], T.xb[:]).then_inc(S.qX, 1)
 
     sent = [0]
 
@@ -102,44 +101,52 @@ def rank_program(g, core, T, topo):
         sent[0] += _count(mask)
         return RemoteDMATransfer(dst_ids=[DstId(rid=rid, pnc=pid)], dma_engine_mask=mask, remote_sem=sem, src=ap, dst=ap)
 
-    p_own = cod(me, 0, TW).bitcast(dt.uint8)
-    a_own = cod(me, TW, AC).bitcast(dt.uint8)
-    b_own = cod(me, AC, WC).bitcast(dt.uint8)
-    s_own = pla(me, 0, WC)
+    def codes(r, a, b):
+        return cod(r, a, b).bitcast(dt.uint8)
+
+    def sem(p, r):
+        return S["s%s%d" % (p, r)]
+
     g.wait_ge(S.qP, 1)
-    g.remote_dma_fused([xfer(peer, R["off"], S["sP%d" % me], p_own),
-                        xfer(nb, R["on"], S["sP%d" % me], p_own)], local_sem=S.ls)
+    g.remote_dma_fused([xfer(peer, R["off"], sem("P", me), codes(me, 0, TW))], local_sem=S.ls)
+    g.remote_dma_fused([xfer(nb, R["on"], sem("P", me), codes(me, 0, TW))], local_sem=S.ls)
     g.wait_ge(S.qA, 1)
-    g.remote_dma_fused([xfer(peer, R["off"], S["sA%d" % me], a_own),
-                        xfer(nb, R["on"], S["sA%d" % me], a_own)], local_sem=S.ls)
+    g.remote_dma_fused([xfer(peer, R["off"], sem("A", me), codes(me, TW, AC)),
+                        xfer(nb, R["on"], sem("A", me), codes(me, TW, AC))], local_sem=S.ls)
     g.wait_ge(S.qT, 1)
     g.wait_ge(S.qW, 1)
-    g.remote_dma_fused([xfer(peer, R["off"], S["sS%d" % me], s_own),
-                        xfer(nb, R["on"], S["sS%d" % me], s_own)], local_sem=S.ls)
-    g.remote_dma_fused([xfer(peer, R["lo"], S["sB%d" % me], b_own),
-                        xfer(diag, R["hi"], S["sB%d" % me], b_own),
-                        xfer(nb, R["on"], S["sB%d" % me], b_own)], local_sem=S.ls)
+    g.remote_dma_fused([xfer(peer, R["off"], sem("S", me), pla(me, 0, WC)),
+                        xfer(nb, R["on"], sem("S", me), pla(me, 0, WC))], local_sem=S.ls)
+    for p, a, b in (("T", AC, 4 * TW), ("W", 4 * TW, WC)):
+        g.remote_dma_fused([xfer(peer, R["lo"], sem(p, me), codes(me, a, b)),
+                            xfer(diag, R["hi"], sem(p, me), codes(me, a, b))], local_sem=S.ls)
+    g.remote_dma_fused([xfer(nb, R["on"], sem("T", me), codes(me, AC, WC))], local_sem=S.ls)
 
     Rn, Rp, Rd = _roles(nb, T.cores, topo), _roles(peer, T.cores, topo), _roles(diag, T.cores, topo)
-    need = {("P", rn): _count(Rn["on"]), ("A", rn): _count(Rn["on"]), ("S", rn): _count(Rn["on"]), ("B", rn): _count(Rn["on"]),
-            ("P", rp): _count(Rp["off"]), ("A", rp): _count(Rp["off"]), ("S", rp): _count(Rp["off"]),
-            ("B", rp): _count(Rp["lo"]),
-            ("A", rd): _count(Rn["on"]), ("S", rd): _count(Rn["on"]), ("B", rd): _count(Rd["hi"])}
+    need = {}
+    for p in "PAST":
+        need[(p, rn)] = _count(Rn["on"])
+    for p in "PAS":
+        need[(p, rp)] = _count(Rp["off"])
+    for p in "AS":
+        need[(p, rd)] = _count(Rn["on"])
+    for p in "TW":
+        need[(p, rp)] = _count(Rp["lo"])
+        need[(p, rd)] = _count(Rd["hi"])
 
-    g.wait_ge(S["sP%d" % rp], need[("P", rp)])
-    g.wait_ge(S["sA%d" % rp], need[("A", rp)])
-    a_peer = cod(rp, 0, AC).bitcast(dt.uint8)
-    g.remote_dma_fused([xfer(nb, R["on"], S["sA%d" % rp], a_peer)], local_sem=S.ls)
-    g.wait_ge(S["sS%d" % rp], need[("S", rp)])
-    g.remote_dma_fused([xfer(nb, R["on"], S["sS%d" % rp], pla(rp, 0, WC))], local_sem=S.ls)
+    g.wait_ge(sem("P", rp), need[("P", rp)])
+    g.wait_ge(sem("A", rp), need[("A", rp)])
+    g.remote_dma_fused([xfer(nb, R["on"], sem("A", rp), codes(rp, 0, AC))], local_sem=S.ls)
+    g.wait_ge(sem("S", rp), need[("S", rp)])
+    g.remote_dma_fused([xfer(nb, R["on"], sem("S", rp), pla(rp, 0, WC))], local_sem=S.ls)
     g.wait_ge(S.ls, sent[0])
 
-    seq = ([("Z", me, i) for i in range(4)] + [("Y", me, 0)]
-           + [("Z", rn, i) for i in range(KA)] + [("Z", rp, i) for i in range(KA)]
-           + [("Z", rn, i) for i in range(KA, 4)] + [("Y", rn, 0)]
+    seq = ([("Z", me, i) for i in range(4)]
+           + [("Z", rn, i) for i in range(KA)] + [("Y", me, 0)]
+           + [("Z", rp, i) for i in range(KA)] + [("Z", rn, KA)]
            + [("Z", rd, i) for i in range(KA)]
-           + [("Z", rp, i) for i in range(KA, 4)] + [("Z", rd, i) for i in range(KA, 4)]
-           + [("Y", rp, 0), ("Y", rd, 0)])
+           + [("Z", rp, KA), ("Z", rd, KA)]
+           + [("Y", rn, 0), ("Y", rp, 0), ("Y", rd, 0)])
     waited = set()
 
     def twait(name, val):
@@ -149,11 +156,13 @@ def rank_program(g, core, T, topo):
 
     def operands(r, piece):
         if r == me:
-            twait({"P": "qP", "A": "qA", "T": "qT", "W": "qW"}[piece], 1)
+            twait("q" + piece, 1)
         else:
-            p = {"P": "P", "A": "A", "T": "B", "W": "B"}[piece]
+            p = piece
             if r == rd and p == "P":
                 p = "A"
+            if r == rn and p == "W":
+                p = "T"
             twait("s%s%d" % (p, r), need[(p, r)])
             twait("sS%d" % r, need[("S", r)])
 

from concourse.bass import DstId, RemoteDMATransfer
from concourse.mybir import dt, AluOpType, ActivationFunctionType

N = 4
NC = 256
TW = 128
WC = 5 * TW
KA = 3
AC = KA * TW
CSCALE = 0.031
ZB = 7

SCRATCH = {
    "w1b": ("sbuf", [128, 4 * 4 * TW], "bfloat16"),
    "w2b": ("sbuf", [128, 4 * TW], "bfloat16"),
    "xb": ("sbuf", [128, 4 * NC], "bfloat16"),
    "xq": ("sbuf", [128, NC], "float8_e4m3fn_x4"),
    "xs": ("sbuf", [128, NC], "uint8"),
    "wq": ("sbuf", [128, N * WC], "float8_e4m3fn_x4"),
    "ws": ("sbuf", [128, N * WC], "uint8"),
    "hb": ("sbuf", [128, N * 4 * NC], "bfloat16"),
    "hq": ("sbuf", [128, N * NC], "float8_e4m3fn_x4"),
    "hs": ("sbuf", [128, N * NC], "uint8"),
    "ysb": ("sbuf", [128, NC], "float32"),
    "ps": ("psum", [128, 512 * (ZB + 1)], "float32"),
}
SEMAPHORES = (["lP", "lA", "lT", "lW", "lX", "qP", "qA", "qT", "qW", "qX", "ls", "yd", "cp", "st"]
              + ["s%s%d" % (p, r) for p in "PASTW" for r in range(N)]
              + ["z%d" % k for k in range(4 * N)] + ["a%d" % k for k in range(4 * N)] + ["hq%d" % r for r in range(N)])


def _engines(mask):
    return [e for e in range(mask.bit_length()) if (mask >> e) & 1]


def _pack(engs):
    m = 0
    for e in engs:
        m |= 1 << e
    return m


def _count(mask):
    return len(_engines(mask))


def _roles(c, cores, topo):
    others = [o for o in cores if o != c]
    nb = [o for o in others if topo.host(o) == topo.host(c) and topo.chip(o) == topo.chip(c)][0]
    far = [o for o in others if o != nb]
    peer = [o for o in far if topo.die(o) == topo.die(c)][0]
    diag = [o for o in far if o != peer][0]
    off = topo.mask(c, peer) & topo.mask(c, diag)
    on = topo.mask(c, nb) & ~off
    e = _engines(off)
    return {"nb": nb, "peer": peer, "diag": diag, "off": off, "on": on,
            "lo": _pack(e[:len(e) // 2]), "hi": _pack(e[len(e) // 2:])}


def rank_program(g, core, T, topo):
    me = T.rank_of(core)
    if me is None:
        return
    S = T.sem
    R = _roles(core, T.cores, topo)
    nb, peer, diag = R["nb"], R["peer"], R["diag"]
    rn, rp, rd = T.rank_of(nb), T.rank_of(peer), T.rank_of(diag)
    v, sc, te = g.vector, g.scalar, g.tensor

    def cod(r, a, b):
        return T.wq[:, WC * r + a:WC * r + b]

    def pla(r, a, b):
        return T.ws[:, WC * r + a:WC * r + b]

    e0, ea = 4 * TW, 4 * AC
    g.sync.dma_start(T.w1b[0:64, 0:e0], T.w1[0:64, 0:e0]).then_inc(S.lP, 16)
    sc.dma_start(T.w1b[64:128, 0:e0], T.w1[64:128, 0:e0]).then_inc(S.lP, 16)
    g.sync.dma_start(T.xb[0:64, :], T.x[0:64, :]).then_inc(S.lX, 16)
    sc.dma_start(T.xb[64:128, :], T.x[64:128, :]).then_inc(S.lX, 16)
    g.sync.dma_start(T.w1b[0:64, e0:ea], T.w1[0:64, e0:ea]).then_inc(S.lA, 16)
    sc.dma_start(T.w1b[64:128, e0:ea], T.w1[64:128, e0:ea]).then_inc(S.lA, 16)
    g.sync.dma_start(T.w1b[:, ea:16 * TW], T.w1[:, ea:16 * TW]).then_inc(S.lT, 16)
    sc.dma_start(T.w2b[:], T.w2[:]).then_inc(S.lW, 16)

    v.wait_ge(S.lP, 32)
    v.quantize_mx(cod(me, 0, TW), pla(me, 0, TW), T.w1b[:, 0:e0]).then_inc(S.qP, 1)
    v.wait_ge(S.lX, 32)
    v.quantize_mx(T.xq[:], T.xs[:], T.xb[:]).then_inc(S.qX, 1)
    v.wait_ge(S.lA, 32)
    v.quantize_mx(cod(me, TW, AC), pla(me, TW, AC), T.w1b[:, e0:ea]).then_inc(S.qA, 1)
    v.wait_ge(S.lT, 16)
    v.quantize_mx(cod(me, AC, 4 * TW), pla(me, AC, 4 * TW), T.w1b[:, ea:16 * TW]).then_inc(S.qT, 1)
    v.wait_ge(S.lW, 16)
    v.quantize_mx(cod(me, 4 * TW, WC), pla(me, 4 * TW, WC), T.w2b[:]).then_inc(S.qW, 1)

    sent = [0]

    def xfer(dst, mask, sem, ap):
        rid, pid = topo.addr(dst, core)
        sent[0] += _count(mask)
        return RemoteDMATransfer(dst_ids=[DstId(rid=rid, pnc=pid)], dma_engine_mask=mask, remote_sem=sem, src=ap, dst=ap)

    def codes(r, a, b):
        return cod(r, a, b).bitcast(dt.uint8)

    def sem(p, r):
        return S["s%s%d" % (p, r)]

    g.wait_ge(S.qP, 1)
    g.remote_dma_fused([xfer(peer, R["off"], sem("P", me), codes(me, 0, TW))], local_sem=S.ls)
    g.remote_dma_fused([xfer(nb, R["on"], sem("P", me), codes(me, 0, TW))], local_sem=S.ls)
    g.wait_ge(S.qA, 1)
    g.remote_dma_fused([xfer(peer, R["off"], sem("A", me), codes(me, TW, AC)),
                        xfer(nb, R["on"], sem("A", me), codes(me, TW, AC))], local_sem=S.ls)
    g.wait_ge(S.qT, 1)
    g.wait_ge(S.qW, 1)
    g.remote_dma_fused([xfer(peer, R["off"], sem("S", me), pla(me, 0, WC)),
                        xfer(nb, R["on"], sem("S", me), pla(me, 0, WC))], local_sem=S.ls)
    for p, a, b in (("T", AC, 4 * TW), ("W", 4 * TW, WC)):
        g.remote_dma_fused([xfer(peer, R["lo"], sem(p, me), codes(me, a, b)),
                            xfer(diag, R["hi"], sem(p, me), codes(me, a, b))], local_sem=S.ls)
    g.remote_dma_fused([xfer(nb, R["on"], sem("T", me), codes(me, AC, WC))], local_sem=S.ls)

    Rn, Rp, Rd = _roles(nb, T.cores, topo), _roles(peer, T.cores, topo), _roles(diag, T.cores, topo)
    need = {}
    for p in "PAST":
        need[(p, rn)] = _count(Rn["on"])
    for p in "PAS":
        need[(p, rp)] = _count(Rp["off"])
    for p in "AS":
        need[(p, rd)] = _count(Rn["on"])
    for p in "TW":
        need[(p, rp)] = _count(Rp["lo"])
        need[(p, rd)] = _count(Rd["hi"])

    g.wait_ge(sem("P", rp), need[("P", rp)])
    g.wait_ge(sem("A", rp), need[("A", rp)])
    g.remote_dma_fused([xfer(nb, R["on"], sem("A", rp), codes(rp, 0, AC))], local_sem=S.ls)
    g.wait_ge(sem("S", rp), need[("S", rp)])
    g.remote_dma_fused([xfer(nb, R["on"], sem("S", rp), pla(rp, 0, WC))], local_sem=S.ls)
    g.wait_ge(S.ls, sent[0])

    seq = ([("Z", me, i) for i in range(4)]
           + [("Z", rn, i) for i in range(KA)] + [("Y", me, 0)]
           + [("Z", rp, i) for i in range(KA)] + [("Z", rn, KA)]
           + [("Z", rd, i) for i in range(KA)]
           + [("Z", rp, KA), ("Z", rd, KA)]
           + [("Y", rn, 0), ("Y", rp, 0), ("Y", rd, 0)])
    waited = set()

    def twait(name, val):
        if name not in waited:
            waited.add(name)
            te.wait_ge(S[name], val)

    def operands(r, piece):
        if r == me:
            twait("q" + piece, 1)
        else:
            p = piece
            if r == rd and p == "P":
                p = "A"
            if r == rn and p == "W":
                p = "T"
            twait("s%s%d" % (p, r), need[(p, r)])
            twait("sS%d" % r, need[("S", r)])

    k = 0
    acts = {r: [] for r in range(N)}
    ny = 0
    ybank = T.ps[:, 512 * ZB:512 * ZB + NC]
    for kind, r, i in seq:
        if kind == "Z":
            twait("qX", 1)
            operands(r, "P" if i == 0 else ("A" if i < KA else "T"))
            if k >= ZB:
                twait("a%d" % (k - ZB), 1)
            bank = T.ps[:, 512 * (k % ZB):512 * (k % ZB) + NC]
            te.matmul_mx(bank, cod(r, TW * i, TW * i + TW), pla(r, TW * i, TW * i + TW),
                         T.xq[:], T.xs[:], True, True).then_inc(S["z%d" % k], 1)
            hv = T.hb[:, 4 * NC * r + i:4 * NC * (r + 1):4]
            if i == 1:
                v.wait_ge(S["z%d" % k], 1)
                v.tensor_scalar(hv, bank, 0.0, CSCALE, AluOpType.max, AluOpType.mult).then_inc(S["a%d" % k], 1)
            else:
                sc.wait_ge(S["z%d" % k], 1)
                sc.activation(hv, bank, ActivationFunctionType.Relu, scale=CSCALE).then_inc(S["a%d" % k], 1)
            acts[r].append(k)
            k += 1
            if len(acts[r]) == 4:
                for j in acts[r]:
                    v.wait_ge(S["a%d" % j], 1)
                v.quantize_mx(T.hq[:, NC * r:NC * (r + 1)], T.hs[:, NC * r:NC * (r + 1)],
                              T.hb[:, 4 * NC * r:4 * NC * (r + 1)]).then_inc(S["hq%d" % r], 1)
        else:
            operands(r, "W")
            twait("hq%d" % r, 1)
            ny += 1
            mm = te.matmul_mx(ybank, cod(r, 4 * TW, WC), pla(r, 4 * TW, WC),
                              T.hq[:, NC * r:NC * (r + 1)], T.hs[:, NC * r:NC * (r + 1)], ny == 1, ny == N)
            if ny == N:
                mm.then_inc(S.yd, 1)

    sc.wait_ge(S.yd, 1)
    sc.activation(T.ysb[:], ybank, ActivationFunctionType.Copy).then_inc(S.cp, 1)
    sc.wait_ge(S.cp, 1)
    sc.dma_start(T.y[:], T.ysb[:]).then_inc(S.st, 16)
    sc.wait_ge(S.st, 16)
